import numpy as np
import ml_dtypes


def mxq(x, axis, fmt="e4m3"):
    dtype, down = {"e4m3": (ml_dtypes.float8_e4m3fn, 7), "e5m2": (ml_dtypes.float8_e5m2, 14)}[fmt]
    v = np.moveaxis(np.asarray(x, np.float32).astype(ml_dtypes.bfloat16).astype(np.float64), axis, -1)
    blocks = v.reshape(v.shape[:-1] + (-1, 32))
    amax = np.abs(blocks).max(-1, keepdims=True)
    byte = np.maximum(np.where(amax > 0, np.frexp(amax)[1] - 1 + 127, 0) - down, 1)
    scale = np.exp2(byte - 127.0)
    codes = (blocks / scale).astype(np.float32).astype(dtype).astype(np.float64)
    return np.moveaxis((codes * scale).reshape(v.shape), -1, axis)


WIDE = False


def mx_kscale(k):
    if not WIDE:
        return np.ones(k)
    levels = np.array([10, -10, 5, -5, 0])
    if k % 512:
        return np.exp2(np.random.permutation(np.resize(levels, k // 32))).repeat(32)
    a = np.empty((k // 512, 16))
    for p in range(k // 512):
        a[p, :8] = np.random.permutation(np.resize(levels, 8))
        for g in range(8):
            far = levels[np.abs(levels - a[p, g]) >= 10]
            a[p, g + 8] = far[np.random.randint(len(far))]
    return np.exp2(a.ravel()).repeat(32)


def f64(x):
    return np.asarray(x).astype(np.float64)


def striped(idx):
    return np.tile(np.asarray(idx).reshape(-1, 16).T, (8, 1)).astype(np.uint16)


def unstriped(offs):
    return offs[:16].T.reshape(-1).astype(np.int64)


E2M1 = np.array([0.0, 0.5, 1.0, 1.5, 2.0, 3.0, 4.0, 6.0, -0.0, -0.5, -1.0, -1.5, -2.0, -3.0, -4.0, -6.0])


def pack_weight(w, fmt):
    k, n = w.shape
    w = f64(np.asarray(w, np.float32).astype(ml_dtypes.bfloat16)).reshape(k // 32, 32, n)
    amax = np.abs(w).max(1)
    if fmt == "e4m3":
        byte = np.frexp(amax)[1] - 1 + 127 - 7
    else:
        mant, ex = np.frexp(amax / 6.0)
        byte = np.where(mant > 0.5, ex, ex - 1) + 127
    byte = np.clip(np.where(amax > 0, byte, 1), 1, 254)
    scaled = (w * np.exp2(127.0 - byte)[:, None, :]).reshape(k, n).astype(np.float32)
    by_word = np.ascontiguousarray(scaled.reshape(k // 512, 128, 4, n).transpose(0, 1, 3, 2))
    if fmt == "e4m3":
        words = by_word.astype(ml_dtypes.float8_e4m3fn).view(np.uint8)
    else:
        c = by_word.astype(ml_dtypes.float4_e2m1fn).view(np.uint8) & 0xF
        words = (c[..., 0::2] | (c[..., 1::2] << 4)).reshape(k // 512, 128, 2 * n)
    return np.ascontiguousarray(words), np.ascontiguousarray(byte.astype(np.uint8).reshape(k // 512, 16, n))


def unpack_weight(words, scales, fmt):
    g, _, n = scales.shape
    words = np.ascontiguousarray(words).reshape(g, 128, n, -1)
    if fmt == "e4m3":
        vals = words.view(ml_dtypes.float8_e4m3fn).astype(np.float64)
    else:
        nib = np.empty((g, 128, n, 4), np.uint8)
        nib[..., 0::2] = words & 0xF
        nib[..., 1::2] = words >> 4
        vals = E2M1[nib]
    vals = vals * np.repeat(np.exp2(scales.astype(np.float64) - 127.0), 8, axis=1)[..., None]
    return vals.transpose(0, 1, 3, 2).reshape(g * 512, n)


def bf(x):
    return np.asarray(x, np.float32).astype(ml_dtypes.bfloat16)


def planes(Y):
    r, m = Y.shape
    b = f64(bf(Y)).reshape(r // 32, 32, m)
    amax = np.abs(b).max(1)
    byte = np.clip(np.where(amax > 0, np.frexp(amax)[1] - 1 + 127 - 7, 1), 1, 254)
    codes = (b * np.exp2(127.0 - byte)[:, None, :]).reshape(r, m).astype(np.float32).astype(ml_dtypes.float8_e4m3fn).view(np.uint8)
    words = codes.reshape(r // 512, 128, 4, m).transpose(0, 1, 3, 2)
    return np.ascontiguousarray(words), np.ascontiguousarray(byte.astype(np.uint8).reshape(r // 512, 16, m))


B, N, T, D, NQ = 1, 512, 2048, 512, 512
DV = 512


def sgn(shape):
    return np.random.uniform(0.5, 2.0, shape) * np.where(np.random.standard_normal(shape) < 0, -1.0, 1.0)


def setup_inputs():
    n = np.random.standard_normal
    pages = np.random.permutation(T // 32)[:B * N // 32]
    idx = (pages[:, None] * 32 + np.arange(32)[None, :]).reshape(-1)
    s = mx_kscale(D)[:, None]
    u = mx_kscale(N)
    ut = np.ones(T)
    ut[idx] = u
    kp = pack_weight(n((D, T)) / s, "e4m3")
    return {
        "qT": (n((B, D, NQ)) * s * (1.00 / np.sqrt(D))).astype(np.float32),
        "k_words": kp[0],
        "k_scales": kp[1],
        "vT": (n((DV, T)) / ut).astype(np.float32),
        "rw": (np.random.uniform(0.05, 0.2, (B, 1, NQ))).astype(np.float32),
        "us": (sgn((B, N, 1)) * u[:, None]).astype(np.float32),
        "offs": striped(idx),
    }


def reference(qT, k_words, k_scales, vT, rw, us, offs):
    idx = unstriped(offs)
    pick = lambda x, which: x[:, which].reshape(x.shape[0], B, -1).transpose(1, 0, 2)
    k = unpack_weight(k_words, k_scales, "e4m3")
    kg = pick(k, idx)
    qq = mxq(f64(qT), 1, "e4m3")
    a = kg.transpose(0, 2, 1) @ qq
    y = np.square(np.maximum(a, 0.0)) * f64(us)
    wq = mxq(y, 1, "e4m3")
    o = mxq(pick(f64(vT), idx).transpose(0, 2, 1), 1, "e4m3").transpose(0, 2, 1) @ wq
    r_ = o * f64(rw)
    Y = r_[0]
    words, scales = planes(Y)
    return Y, words, scales

@@ -1,0 +1,188 @@
+from contextlib import ExitStack
+
+import concourse.mybir as mybir
+from concourse.masks import make_identity
+
+F32 = mybir.dt.float32
+BF16 = mybir.dt.bfloat16
+I32 = mybir.dt.int32
+U32 = mybir.dt.uint32
+U16 = mybir.dt.uint16
+U8 = mybir.dt.uint8
+FP8X4 = mybir.dt.float8_e4m3fn_x4
+ACT = mybir.ActivationFunctionType
+MULT = mybir.AluOpType.mult
+
+P = 128
+PACK = 4
+TOKENS, SLOTS, FEATURES, QUERIES = 2048, 512, 512, 512
+CHUNK = 128
+SCALAR_SHARE = 192
+FLOPS = 2 * 2 * 512 * 512 * 512
+
+
+def interleave(engine_copy, dst, src):
+    engine_copy(out=dst.rearrange("p (c i) t -> p c t i", i=4), in_=src.rearrange("p t (c i) -> p c t i", i=4))
+
+
+def tile_attend_plo_relu2_kernel(tc, qT, k_words, k_scales, vT, rw, us, offs, out_0, out_1, out_2):
+    nc = tc.nc
+    with ExitStack() as ctx:
+        held = ctx.enter_context(tc.tile_pool(name="held", bufs=1))
+        ring = ctx.enter_context(tc.tile_pool(name="ring", bufs=2))
+        banks = ctx.enter_context(tc.psum_pool(name="banks", bufs=6))
+        turns = ctx.enter_context(tc.psum_pool(name="turns", bufs=2))
+
+        offsets = held.tile([P, SLOTS // 16], U16, name="offsets")
+        nc.sync.dma_start(offsets[:], offs)
+
+        slot_scale = held.tile([P, PACK], F32, name="slot_scale")
+        nc.sync.dma_start(out=slot_scale[:], in_=us[0].rearrange("(p r) o -> p (r o)", r=PACK))
+        row_scale_cols = held.tile([P, PACK], F32, name="row_scale_cols")
+        nc.sync.dma_start(out=row_scale_cols[:], in_=rw[0].rearrange("o (p c) -> p (o c)", c=PACK))
+        key_scale_pool = held.tile([P, TOKENS], U8, name="key_scale_pool", tag="wide1", align_bytes=64)
+        nc.gpsimd.memset(key_scale_pool[:].bitcast(I32), 0)
+        for quad in range(4):
+            nc.scalar.dma_start(out=key_scale_pool[32 * quad : 32 * quad + 4, :].bitcast(I32),
+                                in_=k_scales[0, 4 * quad : 4 * quad + 4, :].bitcast(I32))
+
+        q_raw = held.tile([P, PACK, QUERIES], F32, name="q_raw", tag="wide2", align_bytes=64)
+        nc.sync.dma_start(out=q_raw[:], in_=qT[0].rearrange("(p j) q -> p j q", j=PACK))
+        key_pool = held.tile([P, TOKENS], I32, name="key_pool", tag="wide3", align_bytes=64)
+        nc.sync.dma_start(out=key_pool[:], in_=k_words[0].rearrange("p t r -> p (t r)").bitcast(I32))
+        value_rows = vT.rearrange("(p t) n -> t p n", t=PACK)
+        value_pools = []
+
+        def load_values(t):
+            value_pool = held.tile([P, TOKENS], F32, name="value_pool", tag="wide%d" % t, align_bytes=64)
+            nc.sync.dma_start(out=value_pool[:], in_=value_rows[t])
+            value_pools.append(value_pool)
+
+        load_values(0)
+
+        identity = held.tile([P, P], F32, name="identity", align_bytes=64)
+        make_identity(nc, identity[:])
+
+        spread = banks.tile([P, PACK, P], F32, name="spread", tag="bank")
+        for c in range(PACK):
+            nc.tensor.transpose(spread[:, c, :], row_scale_cols[:, c : c + 1].to_broadcast([P, P]), identity[:])
+        row_scale = held.tile([P, QUERIES], F32, name="row_scale", align_bytes=64)
+        nc.scalar.activation(out=row_scale[:].rearrange("p (n c) -> p n c", c=PACK),
+                             in_=spread[:].rearrange("p c n -> p n c"), func=ACT.Copy)
+
+        listed_scales = held.tile([P, SLOTS], U8, name="listed_scales", tag="listed_keys", align_bytes=64)
+        nc.vector.tensor_copy(out=listed_scales[:], in_=key_scale_pool[:].indirect(offsets[:]))
+        key_scales = held.tile([P, SLOTS], U8, name="key_scales", align_bytes=64)
+        nc.vector.tensor_copy(out=key_scales[:].rearrange("p (r s) -> p r s", r=PACK),
+                              in_=listed_scales[:].rearrange("p (s r) -> p r s", r=PACK))
+        q_codes = held.tile([P, QUERIES], U32, name="q_codes", align_bytes=64)
+        q_scales = held.tile([P, QUERIES], U8, name="q_scales", align_bytes=64)
+        y_codes = held.tile([P, QUERIES], U32, name="y_codes", align_bytes=64)
+        y_scales = held.tile([P, QUERIES], U8, name="y_scales", align_bytes=64)
+        chunks = [slice(c * CHUNK, (c + 1) * CHUNK) for c in range(QUERIES // CHUNK)]
+        q_bf = []
+        for c, cols in enumerate(chunks):
+            grouped = held.tile([P, CHUNK, PACK], BF16, name="q_bf%d" % c, align_bytes=64)
+            interleave(nc.scalar.copy, grouped[:], q_raw[:, :, cols])
+            q_bf.append(grouped)
+        for c, cols in enumerate(chunks):
+            nc.vector.quantize_mx(out=q_codes[:, cols].bitcast(FP8X4), scales=q_scales[:, cols],
+                                  in_=q_bf[c][:].rearrange("p q j -> p (q j)"))
+
+        key_codes = held.tile([P, SLOTS], I32, name="key_codes", tag="listed_keys", align_bytes=64)
+        nc.vector.tensor_copy(out=key_codes[:].bitcast(U32).rearrange("p (r s) -> p s r", r=PACK),
+                              in_=key_pool[:].bitcast(U32).indirect(offsets[:]))
+
+        for t in range(1, PACK):
+            load_values(t)
+
+        result = held.tile([P, PACK, QUERIES], F32, name="result", align_bytes=64)
+        out_rows = out_0.rearrange("(p t) q -> p t q", t=PACK)
+        value_codes = held.tile([P, PACK, P], U32, name="value_codes", align_bytes=64)
+        value_scales = held.tile([P, PACK, P], U8, name="value_scales", align_bytes=64)
+
+        def weigh(c):
+            cols = chunks[c]
+            scores = banks.tile([P, PACK, CHUNK], F32, name="scores", tag="bank")
+            for r in range(PACK):
+                keys = slice(r * P, (r + 1) * P)
+                nc.tensor.matmul_mx(out=scores[:, r, :], lhsT=key_codes[:, keys].bitcast(FP8X4),
+                                    lhsT_scale=key_scales[:, keys], rhs=q_codes[:, cols].bitcast(FP8X4),
+                                    rhs_scale=q_scales[:, cols], start=True, stop=True)
+            positive = ring.tile([P, CHUNK, PACK], F32, name="positive", align_bytes=64)
+            nc.scalar.activation(out=positive[:], in_=scores[:].rearrange("p r q -> p q r"), func=ACT.Relu)
+            squared = ring.tile([P, CHUNK, PACK], F32, name="squared", align_bytes=64)
+            nc.scalar.activation(out=squared[:], in_=positive[:], func=ACT.Square)
+            weights = held.tile([P, CHUNK, PACK], BF16, name="weights%d" % c, align_bytes=64)
+            nc.vector.tensor_tensor(out=weights[:], in0=squared[:],
+                                    in1=slot_scale[:].unsqueeze(1).to_broadcast([P, CHUNK, PACK]), op=MULT)
+            return weights
+
+        def quantise_weights(c, weights):
+            cols = chunks[c]
+            nc.vector.quantize_mx(out=y_codes[:, cols].bitcast(FP8X4), scales=y_scales[:, cols],
+                                  in_=weights[:].rearrange("p q r -> p (q r)"))
+
+        def gather_values(t):
+            listed = ring.tile([P, SLOTS], BF16, name="listed", align_bytes=64)
+            nc.vector.tensor_copy(out=listed[:], in_=value_pools[t][:].indirect(offsets[:]))
+            words = listed[:].bitcast(F32)
+            turned = turns.tile([P, 2, P], F32, name="turned")
+            for u in range(2):
+                nc.tensor.transpose(turned[:, u, :], words[:, u : 2 * P : 2], identity[:])
+            grouped = ring.tile([P, P * PACK], BF16, name="v_bf", align_bytes=64)
+            nc.scalar.copy(out=grouped[:].bitcast(F32).rearrange("p (f u) -> p f u", u=2),
+                           in_=turned[:].rearrange("p u f -> p f u"))
+            return grouped
+
+        def quantise_values(t, grouped):
+            nc.vector.quantize_mx(out=value_codes[:, t, :].bitcast(FP8X4), scales=value_scales[:, t, :], in_=grouped[:])
+
+        def multiply(t, cols):
+            width = cols.stop - cols.start
+            acc = banks.tile([P, width], F32, name="acc", tag="bank")
+            nc.tensor.matmul_mx(out=acc[:], lhsT=value_codes[:, t, :].bitcast(FP8X4), lhsT_scale=value_scales[:, t, :],
+                                rhs=y_codes[:, cols].bitcast(FP8X4), rhs_scale=y_scales[:, cols], start=True, stop=True)
+            nc.vector.tensor_tensor(out=result[:, t, cols], in0=acc[:], in1=row_scale[:, cols], op=MULT)
+
+        w0 = weigh(0)
+        g0 = gather_values(0)
+        w1 = weigh(1)
+        quantise_weights(0, w0)
+        w2 = weigh(2)
+        quantise_weights(1, w1)
+        quantise_values(0, g0)
+        w3 = weigh(3)
+        quantise_weights(2, w2)
+        g1 = gather_values(1)
+        quantise_weights(3, w3)
+        g2 = gather_values(2)
+        quantise_values(1, g1)
+        every = slice(0, QUERIES)
+        multiply(0, every)
+        quantise_values(2, g2)
+        g3 = gather_values(3)
+        multiply(1, every)
+        nc.sync.dma_start(out=out_rows[:, 0:2, :], in_=result[:, 0:2, :])
+        quantise_values(3, g3)
+        multiply(2, every)
+        nc.sync.dma_start(out=out_rows[:, 2, :], in_=result[:, 2, :])
+        halves = [slice(0, 256), slice(256, 512)]
+        multiply(3, halves[0])
+        multiply(3, halves[1])
+        nc.sync.dma_start(out=out_rows[:, 3, :], in_=result[:, 3, :])
+
+        out_codes = held.tile([P, QUERIES], I32, name="out_codes", align_bytes=64)
+        out_scales = held.tile([P, QUERIES], U8, name="out_scales", align_bytes=64)
+        rounded = held.tile([P, QUERIES, PACK], BF16, name="rounded", align_bytes=64)
+        interleave(nc.scalar.copy, rounded[:, :SCALAR_SHARE, :], result[:, :, :SCALAR_SHARE])
+        interleave(nc.vector.tensor_copy, rounded[:, SCALAR_SHARE:, :], result[:, :, SCALAR_SHARE:])
+        words_out = out_1[0].rearrange("p q t -> p (q t)").bitcast(I32)
+        for cols in reversed(halves):
+            nc.vector.quantize_mx(out=out_codes[:, cols].bitcast(FP8X4), scales=out_scales[:, cols],
+                                  in_=rounded[:, cols, :].rearrange("p q t -> p (q t)"))
+            nc.sync.dma_start(out=words_out[:, cols], in_=out_codes[:, cols])
+        for quad in range(4):
+            engine = nc.scalar if quad % 2 == 0 else nc.sync
+            engine.dma_start(out=out_2[0, 4 * quad : 4 * quad + 4, :].bitcast(I32),
+                             in_=out_scales[32 * quad : 32 * quad + 4, :].bitcast(I32))

@@ -16,7 +16,8 @@ MULT = mybir.AluOpType.mult
 P = 128
 PACK = 4
 TOKENS, SLOTS, FEATURES, QUERIES = 2048, 512, 512, 512
-CHUNK = 128
+HALF = 256
+ROW = 4 * TOKENS
 SCALAR_SHARE = 192
 FLOPS = 2 * 2 * 512 * 512 * 512
 
@@ -29,9 +30,8 @@ def tile_attend_plo_relu2_kernel(tc, qT, k_words, k_scales, vT, rw, us, offs, ou
     nc = tc.nc
     with ExitStack() as ctx:
         held = ctx.enter_context(tc.tile_pool(name="held", bufs=1))
-        ring = ctx.enter_context(tc.tile_pool(name="ring", bufs=2))
-        banks = ctx.enter_context(tc.psum_pool(name="banks", bufs=6))
-        turns = ctx.enter_context(tc.psum_pool(name="turns", bufs=2))
+        shared = ctx.enter_context(tc.tile_pool(name="shared", bufs=1))
+        banks = ctx.enter_context(tc.psum_pool(name="banks", bufs=1))
 
         offsets = held.tile([P, SLOTS // 16], U16, name="offsets")
         nc.sync.dma_start(offsets[:], offs)
@@ -40,21 +40,21 @@ def tile_attend_plo_relu2_kernel(tc, qT, k_words, k_scales, vT, rw, us, offs, ou
         nc.sync.dma_start(out=slot_scale[:], in_=us[0].rearrange("(p r) o -> p (r o)", r=PACK))
         row_scale_cols = held.tile([P, PACK], F32, name="row_scale_cols")
         nc.sync.dma_start(out=row_scale_cols[:], in_=rw[0].rearrange("o (p c) -> p (o c)", c=PACK))
-        key_scale_pool = held.tile([P, TOKENS], U8, name="key_scale_pool", tag="wide1", align_bytes=64)
+        key_scale_pool = shared.tile([P, TOKENS], U8, name="key_scale_pool", offset=ROW, align_bytes=64)
         nc.gpsimd.memset(key_scale_pool[:].bitcast(I32), 0)
         for quad in range(4):
             nc.scalar.dma_start(out=key_scale_pool[32 * quad : 32 * quad + 4, :].bitcast(I32),
                                 in_=k_scales[0, 4 * quad : 4 * quad + 4, :].bitcast(I32))
 
-        q_raw = held.tile([P, PACK, QUERIES], F32, name="q_raw", tag="wide2", align_bytes=64)
+        q_raw = shared.tile([P, PACK, QUERIES], F32, name="q_raw", offset=2 * ROW, align_bytes=64)
         nc.sync.dma_start(out=q_raw[:], in_=qT[0].rearrange("(p j) q -> p j q", j=PACK))
-        key_pool = held.tile([P, TOKENS], I32, name="key_pool", tag="wide3", align_bytes=64)
+        key_pool = shared.tile([P, TOKENS], I32, name="key_pool", offset=3 * ROW, align_bytes=64)
         nc.sync.dma_start(out=key_pool[:], in_=k_words[0].rearrange("p t r -> p (t r)").bitcast(I32))
         value_rows = vT.rearrange("(p t) n -> t p n", t=PACK)
         value_pools = []
 
         def load_values(t):
-            value_pool = held.tile([P, TOKENS], F32, name="value_pool", tag="wide%d" % t, align_bytes=64)
+            value_pool = shared.tile([P, TOKENS], F32, name="value_pool%d" % t, offset=t * ROW, align_bytes=64)
             nc.sync.dma_start(out=value_pool[:], in_=value_rows[t])
             value_pools.append(value_pool)
 
@@ -63,7 +63,16 @@ def tile_attend_plo_relu2_kernel(tc, qT, k_words, k_scales, vT, rw, us, offs, ou
         identity = held.tile([P, P], F32, name="identity", align_bytes=64)
         make_identity(nc, identity[:])
 
-        spread = banks.tile([P, PACK, P], F32, name="spread", tag="bank")
+        slot_sign = held.tile([P, PACK], BF16, name="slot_sign")
+        nc.scalar.activation(out=slot_sign[:], in_=slot_scale[:], func=ACT.Sign)
+        slot_size = held.tile([P, PACK], F32, name="slot_size")
+        nc.scalar.activation(out=slot_size[:], in_=slot_scale[:], func=ACT.Abs)
+        half = held.tile([P, PACK], F32, name="half")
+        nc.gpsimd.memset(half[:], 0.5)
+        slot_root = held.tile([P, PACK], F32, name="slot_root")
+        nc.gpsimd.tensor_tensor(out=slot_root[:], in0=slot_size[:], in1=half[:], op=mybir.AluOpType.pow)
+
+        spread = banks.tile([P, PACK, P], F32, name="spread", tag="bank4")
         for c in range(PACK):
             nc.tensor.transpose(spread[:, c, :], row_scale_cols[:, c : c + 1].to_broadcast([P, P]), identity[:])
         row_scale = held.tile([P, QUERIES], F32, name="row_scale", align_bytes=64)
@@ -79,108 +88,117 @@ def tile_attend_plo_relu2_kernel(tc, qT, k_words, k_scales, vT, rw, us, offs, ou
         q_scales = held.tile([P, QUERIES], U8, name="q_scales", align_bytes=64)
         y_codes = held.tile([P, QUERIES], U32, name="y_codes", align_bytes=64)
         y_scales = held.tile([P, QUERIES], U8, name="y_scales", align_bytes=64)
-        chunks = [slice(c * CHUNK, (c + 1) * CHUNK) for c in range(QUERIES // CHUNK)]
+        halves = [slice(0, HALF), slice(HALF, QUERIES)]
         q_bf = []
-        for c, cols in enumerate(chunks):
-            grouped = held.tile([P, CHUNK, PACK], BF16, name="q_bf%d" % c, align_bytes=64)
+        for h, cols in enumerate(halves):
+            grouped = held.tile([P, HALF, PACK], BF16, name="q_bf%d" % h, align_bytes=64)
             interleave(nc.scalar.copy, grouped[:], q_raw[:, :, cols])
             q_bf.append(grouped)
-        for c, cols in enumerate(chunks):
-            nc.vector.quantize_mx(out=q_codes[:, cols].bitcast(FP8X4), scales=q_scales[:, cols],
-                                  in_=q_bf[c][:].rearrange("p q j -> p (q j)"))
 
+        def quantise(codes, scales, grouped):
+            nc.vector.quantize_mx(out=codes.bitcast(FP8X4), scales=scales, in_=grouped.rearrange("p c t -> p (c t)"))
+
+        quantise(q_codes[:, halves[0]], q_scales[:, halves[0]], q_bf[0][:])
         key_codes = held.tile([P, SLOTS], I32, name="key_codes", tag="listed_keys", align_bytes=64)
         nc.vector.tensor_copy(out=key_codes[:].bitcast(U32).rearrange("p (r s) -> p s r", r=PACK),
                               in_=key_pool[:].bitcast(U32).indirect(offsets[:]))
+        quantise(q_codes[:, halves[1]], q_scales[:, halves[1]], q_bf[1][:])
 
         for t in range(1, PACK):
             load_values(t)
 
-        result = held.tile([P, PACK, QUERIES], F32, name="result", align_bytes=64)
         out_rows = out_0.rearrange("(p t) q -> p t q", t=PACK)
         value_codes = held.tile([P, PACK, P], U32, name="value_codes", align_bytes=64)
         value_scales = held.tile([P, PACK, P], U8, name="value_scales", align_bytes=64)
 
-        def weigh(c):
-            cols = chunks[c]
-            scores = banks.tile([P, PACK, CHUNK], F32, name="scores", tag="bank")
+        def square(out, in_):
+            nc.scalar.activation(out=out, in_=in_, func=ACT.Square)
+
+        def weigh(h):
+            cols = halves[h]
+            rooted = held.tile([P, PACK, HALF], F32, name="rooted%d" % h, align_bytes=64)
             for r in range(PACK):
                 keys = slice(r * P, (r + 1) * P)
-                nc.tensor.matmul_mx(out=scores[:, r, :], lhsT=key_codes[:, keys].bitcast(FP8X4),
-                                    lhsT_scale=key_scales[:, keys], rhs=q_codes[:, cols].bitcast(FP8X4),
-                                    rhs_scale=q_scales[:, cols], start=True, stop=True)
-            positive = ring.tile([P, CHUNK, PACK], F32, name="positive", align_bytes=64)
-            nc.scalar.activation(out=positive[:], in_=scores[:].rearrange("p r q -> p q r"), func=ACT.Relu)
-            squared = ring.tile([P, CHUNK, PACK], F32, name="squared", align_bytes=64)
-            nc.scalar.activation(out=squared[:], in_=positive[:], func=ACT.Square)
-            weights = held.tile([P, CHUNK, PACK], BF16, name="weights%d" % c, align_bytes=64)
-            nc.vector.tensor_tensor(out=weights[:], in0=squared[:],
-                                    in1=slot_scale[:].unsqueeze(1).to_broadcast([P, CHUNK, PACK]), op=MULT)
+                scores = banks.tile([P, HALF], F32, name="scores", tag="bank%d" % (PACK * h + r))
+                nc.tensor.matmul_mx(out=scores[:], lhsT=key_codes[:, keys].bitcast(FP8X4), lhsT_scale=key_scales[:, keys],
+                                    rhs=q_codes[:, cols].bitcast(FP8X4), rhs_scale=q_scales[:, cols], start=True, stop=True)
+                nc.scalar.activation(out=rooted[:, r, :], in_=scores[:], func=ACT.Relu, scale=slot_root[:, r : r + 1])
+            sizes = held.tile([P, HALF, PACK], BF16, name="sizes%d" % h, align_bytes=64)
+            interleave(square, sizes[:], rooted[:])
+            return sizes
+
+        def sign_weights(h, sizes):
+            weights = shared.tile([P, HALF, PACK], BF16, name="weights%d" % h, offset=(h + 1) * ROW + 2048, align_bytes=64)
+            nc.vector.tensor_tensor(out=weights[:], in0=sizes[:],
+                                    in1=slot_sign[:].unsqueeze(1).to_broadcast([P, HALF, PACK]), op=MULT)
             return weights
 
-        def quantise_weights(c, weights):
-            cols = chunks[c]
-            nc.vector.quantize_mx(out=y_codes[:, cols].bitcast(FP8X4), scales=y_scales[:, cols],
-                                  in_=weights[:].rearrange("p q r -> p (q r)"))
+        def quantise_weights(h, weights):
+            quantise(y_codes[:, halves[h]], y_scales[:, halves[h]], weights[:])
 
-        def gather_values(t):
-            listed = ring.tile([P, SLOTS], BF16, name="listed", align_bytes=64)
+        def gather_values(t, bank):
+            listed = held.tile([P, SLOTS], BF16, name="listed%d" % t, align_bytes=64)
             nc.vector.tensor_copy(out=listed[:], in_=value_pools[t][:].indirect(offsets[:]))
             words = listed[:].bitcast(F32)
-            turned = turns.tile([P, 2, P], F32, name="turned")
+            turned = banks.tile([P, 2, P], F32, name="turned", tag=bank)
             for u in range(2):
                 nc.tensor.transpose(turned[:, u, :], words[:, u : 2 * P : 2], identity[:])
-            grouped = ring.tile([P, P * PACK], BF16, name="v_bf", align_bytes=64)
-            nc.scalar.copy(out=grouped[:].bitcast(F32).rearrange("p (f u) -> p f u", u=2),
+            return turned
+
+        def regroup_values(t, turned):
+            place = (2 * ROW, 2 * ROW + 1024, 3 * ROW, 4 * ROW + 1024)[t]
+            grouped = shared.tile([P, P, PACK], BF16, name="v_bf%d" % t, offset=place, align_bytes=64)
+            nc.scalar.copy(out=grouped[:].rearrange("p f t -> p (f t)").bitcast(F32).rearrange("p (f u) -> p f u", u=2),
                            in_=turned[:].rearrange("p u f -> p f u"))
             return grouped
 
         def quantise_values(t, grouped):
-            nc.vector.quantize_mx(out=value_codes[:, t, :].bitcast(FP8X4), scales=value_scales[:, t, :], in_=grouped[:])
+            quantise(value_codes[:, t, :], value_scales[:, t, :], grouped[:])
 
-        def multiply(t, cols):
+        def multiply(t, cols, result, bank):
             width = cols.stop - cols.start
-            acc = banks.tile([P, width], F32, name="acc", tag="bank")
+            acc = banks.tile([P, width], F32, name="acc", tag=bank)
             nc.tensor.matmul_mx(out=acc[:], lhsT=value_codes[:, t, :].bitcast(FP8X4), lhsT_scale=value_scales[:, t, :],
                                 rhs=y_codes[:, cols].bitcast(FP8X4), rhs_scale=y_scales[:, cols], start=True, stop=True)
             nc.vector.tensor_tensor(out=result[:, t, cols], in0=acc[:], in1=row_scale[:, cols], op=MULT)
 
-        w0 = weigh(0)
-        g0 = gather_values(0)
-        w1 = weigh(1)
-        quantise_weights(0, w0)
-        w2 = weigh(2)
-        quantise_weights(1, w1)
+        s0 = weigh(0)
+        t0 = gather_values(0, "bank0")
+        s1 = weigh(1)
+        t1 = gather_values(1, "bank1")
+        quantise_weights(0, sign_weights(0, s0))
+        t2 = gather_values(2, "bank2")
+        g0 = regroup_values(0, t0)
+        g1 = regroup_values(1, t1)
+        w1 = sign_weights(1, s1)
         quantise_values(0, g0)
-        w3 = weigh(3)
-        quantise_weights(2, w2)
-        g1 = gather_values(1)
-        quantise_weights(3, w3)
-        g2 = gather_values(2)
         quantise_values(1, g1)
-        every = slice(0, QUERIES)
-        multiply(0, every)
+        quantise_weights(1, w1)
+        t3 = gather_values(3, "bank3")
+        g2 = regroup_values(2, t2)
+        g3 = regroup_values(3, t3)
         quantise_values(2, g2)
-        g3 = gather_values(3)
-        multiply(1, every)
+        result = shared.tile([P, PACK, QUERIES], F32, name="result", offset=3 * ROW + 1024, align_bytes=64)
+        every = slice(0, QUERIES)
+        multiply(0, every, result, "bank4")
+        multiply(1, every, result, "bank5")
         nc.sync.dma_start(out=out_rows[:, 0:2, :], in_=result[:, 0:2, :])
         quantise_values(3, g3)
-        multiply(2, every)
+        multiply(2, every, result, "bank6")
         nc.sync.dma_start(out=out_rows[:, 2, :], in_=result[:, 2, :])
-        halves = [slice(0, 256), slice(256, 512)]
-        multiply(3, halves[0])
-        multiply(3, halves[1])
+        multiply(3, halves[0], result, "bank7")
+        multiply(3, halves[1], result, "bank0")
         nc.sync.dma_start(out=out_rows[:, 3, :], in_=result[:, 3, :])
 
         out_codes = held.tile([P, QUERIES], I32, name="out_codes", align_bytes=64)
         out_scales = held.tile([P, QUERIES], U8, name="out_scales", align_bytes=64)
         rounded = held.tile([P, QUERIES, PACK], BF16, name="rounded", align_bytes=64)
         interleave(nc.scalar.copy, rounded[:, :SCALAR_SHARE, :], result[:, :, :SCALAR_SHARE])
-        interleave(nc.vector.tensor_copy, rounded[:, SCALAR_SHARE:, :], result[:, :, SCALAR_SHARE:])
+        interleave(nc.vector.tensor_copy, rounded[:, SCALAR_SHARE:HALF, :], result[:, :, SCALAR_SHARE:HALF])
+        interleave(nc.vector.tensor_copy, rounded[:, HALF:, :], result[:, :, HALF:])
         words_out = out_1[0].rearrange("p q t -> p (q t)").bitcast(I32)
-        for cols in reversed(halves):
-            nc.vector.quantize_mx(out=out_codes[:, cols].bitcast(FP8X4), scales=out_scales[:, cols],
-                                  in_=rounded[:, cols, :].rearrange("p q t -> p (q t)"))
+        for cols in halves:
+            quantise(out_codes[:, cols], out_scales[:, cols], rounded[:, cols, :])
             nc.sync.dma_start(out=words_out[:, cols], in_=out_codes[:, cols])
         for quad in range(4):
             engine = nc.scalar if quad % 2 == 0 else nc.sync

from contextlib import ExitStack

import concourse.mybir as mybir
from concourse.masks import make_identity

F32 = mybir.dt.float32
BF16 = mybir.dt.bfloat16
I32 = mybir.dt.int32
U32 = mybir.dt.uint32
U16 = mybir.dt.uint16
U8 = mybir.dt.uint8
FP8X4 = mybir.dt.float8_e4m3fn_x4
ACT = mybir.ActivationFunctionType
MULT = mybir.AluOpType.mult

P = 128
PACK = 4
TOKENS, SLOTS, FEATURES, QUERIES = 2048, 512, 512, 512
HALF = 256
ROW = 4 * TOKENS
SCALAR_SHARE = 192
FLOPS = 2 * 2 * 512 * 512 * 512


def interleave(engine_copy, dst, src):
    engine_copy(out=dst.rearrange("p (c i) t -> p c t i", i=4), in_=src.rearrange("p t (c i) -> p c t i", i=4))


def tile_attend_plo_relu2_kernel(tc, qT, k_words, k_scales, vT, rw, us, offs, out_0, out_1, out_2):
    nc = tc.nc
    with ExitStack() as ctx:
        held = ctx.enter_context(tc.tile_pool(name="held", bufs=1))
        shared = ctx.enter_context(tc.tile_pool(name="shared", bufs=1))
        banks = ctx.enter_context(tc.psum_pool(name="banks", bufs=1))

        offsets = held.tile([P, SLOTS // 16], U16, name="offsets")
        nc.sync.dma_start(offsets[:], offs)

        slot_scale = held.tile([P, PACK], F32, name="slot_scale")
        nc.sync.dma_start(out=slot_scale[:], in_=us[0].rearrange("(p r) o -> p (r o)", r=PACK))
        row_scale_cols = held.tile([P, PACK], F32, name="row_scale_cols")
        nc.sync.dma_start(out=row_scale_cols[:], in_=rw[0].rearrange("o (p c) -> p (o c)", c=PACK))
        key_scale_pool = shared.tile([P, TOKENS], U8, name="key_scale_pool", offset=ROW, align_bytes=64)
        nc.gpsimd.memset(key_scale_pool[:].bitcast(I32), 0)
        for quad in range(4):
            nc.scalar.dma_start(out=key_scale_pool[32 * quad : 32 * quad + 4, :].bitcast(I32),
                                in_=k_scales[0, 4 * quad : 4 * quad + 4, :].bitcast(I32))

        q_raw = shared.tile([P, PACK, QUERIES], F32, name="q_raw", offset=2 * ROW, align_bytes=64)
        nc.sync.dma_start(out=q_raw[:], in_=qT[0].rearrange("(p j) q -> p j q", j=PACK))
        key_pool = shared.tile([P, TOKENS], I32, name="key_pool", offset=3 * ROW, align_bytes=64)
        nc.sync.dma_start(out=key_pool[:], in_=k_words[0].rearrange("p t r -> p (t r)").bitcast(I32))
        value_rows = vT.rearrange("(p t) n -> t p n", t=PACK)
        value_pools = []

        def load_values(t):
            value_pool = shared.tile([P, TOKENS], F32, name="value_pool%d" % t, offset=t * ROW, align_bytes=64)
            nc.sync.dma_start(out=value_pool[:], in_=value_rows[t])
            value_pools.append(value_pool)

        load_values(0)

        identity = held.tile([P, P], F32, name="identity", align_bytes=64)
        make_identity(nc, identity[:])

        slot_sign = held.tile([P, PACK], BF16, name="slot_sign")
        nc.scalar.activation(out=slot_sign[:], in_=slot_scale[:], func=ACT.Sign)
        slot_size = held.tile([P, PACK], F32, name="slot_size")
        nc.scalar.activation(out=slot_size[:], in_=slot_scale[:], func=ACT.Abs)
        half = held.tile([P, PACK], F32, name="half")
        nc.gpsimd.memset(half[:], 0.5)
        slot_root = held.tile([P, PACK], F32, name="slot_root")
        nc.gpsimd.tensor_tensor(out=slot_root[:], in0=slot_size[:], in1=half[:], op=mybir.AluOpType.pow)

        spread = banks.tile([P, PACK, P], F32, name="spread", tag="bank4")
        for c in range(PACK):
            nc.tensor.transpose(spread[:, c, :], row_scale_cols[:, c : c + 1].to_broadcast([P, P]), identity[:])
        row_scale = held.tile([P, QUERIES], F32, name="row_scale", align_bytes=64)
        nc.scalar.activation(out=row_scale[:].rearrange("p (n c) -> p n c", c=PACK),
                             in_=spread[:].rearrange("p c n -> p n c"), func=ACT.Copy)

        listed_scales = held.tile([P, SLOTS], U8, name="listed_scales", tag="listed_keys", align_bytes=64)
        nc.vector.tensor_copy(out=listed_scales[:], in_=key_scale_pool[:].indirect(offsets[:]))
        key_scales = held.tile([P, SLOTS], U8, name="key_scales", align_bytes=64)
        nc.vector.tensor_copy(out=key_scales[:].rearrange("p (r s) -> p r s", r=PACK),
                              in_=listed_scales[:].rearrange("p (s r) -> p r s", r=PACK))
        q_codes = held.tile([P, QUERIES], U32, name="q_codes", align_bytes=64)
        q_scales = held.tile([P, QUERIES], U8, name="q_scales", align_bytes=64)
        y_codes = held.tile([P, QUERIES], U32, name="y_codes", align_bytes=64)
        y_scales = held.tile([P, QUERIES], U8, name="y_scales", align_bytes=64)
        halves = [slice(0, HALF), slice(HALF, QUERIES)]
        q_bf = []
        for h, cols in enumerate(halves):
            grouped = held.tile([P, HALF, PACK], BF16, name="q_bf%d" % h, align_bytes=64)
            interleave(nc.scalar.copy, grouped[:], q_raw[:, :, cols])
            q_bf.append(grouped)

        def quantise(codes, scales, grouped):
            nc.vector.quantize_mx(out=codes.bitcast(FP8X4), scales=scales, in_=grouped.rearrange("p c t -> p (c t)"))

        quantise(q_codes[:, halves[0]], q_scales[:, halves[0]], q_bf[0][:])
        key_codes = held.tile([P, SLOTS], I32, name="key_codes", tag="listed_keys", align_bytes=64)
        nc.vector.tensor_copy(out=key_codes[:].bitcast(U32).rearrange("p (r s) -> p s r", r=PACK),
                              in_=key_pool[:].bitcast(U32).indirect(offsets[:]))
        quantise(q_codes[:, halves[1]], q_scales[:, halves[1]], q_bf[1][:])

        for t in range(1, PACK):
            load_values(t)

        out_rows = out_0.rearrange("(p t) q -> p t q", t=PACK)
        value_codes = held.tile([P, PACK, P], U32, name="value_codes", align_bytes=64)
        value_scales = held.tile([P, PACK, P], U8, name="value_scales", align_bytes=64)

        def square(out, in_):
            nc.scalar.activation(out=out, in_=in_, func=ACT.Square)

        def weigh(h):
            cols = halves[h]
            rooted = held.tile([P, PACK, HALF], F32, name="rooted%d" % h, align_bytes=64)
            for r in range(PACK):
                keys = slice(r * P, (r + 1) * P)
                scores = banks.tile([P, HALF], F32, name="scores", tag="bank%d" % (PACK * h + r))
                nc.tensor.matmul_mx(out=scores[:], lhsT=key_codes[:, keys].bitcast(FP8X4), lhsT_scale=key_scales[:, keys],
                                    rhs=q_codes[:, cols].bitcast(FP8X4), rhs_scale=q_scales[:, cols], start=True, stop=True)
                nc.scalar.activation(out=rooted[:, r, :], in_=scores[:], func=ACT.Relu, scale=slot_root[:, r : r + 1])
            sizes = held.tile([P, HALF, PACK], BF16, name="sizes%d" % h, align_bytes=64)
            interleave(square, sizes[:], rooted[:])
            return sizes

        def sign_weights(h, sizes):
            weights = shared.tile([P, HALF, PACK], BF16, name="weights%d" % h, offset=(h + 1) * ROW + 2048, align_bytes=64)
            nc.vector.tensor_tensor(out=weights[:], in0=sizes[:],
                                    in1=slot_sign[:].unsqueeze(1).to_broadcast([P, HALF, PACK]), op=MULT)
            return weights

        def quantise_weights(h, weights):
            quantise(y_codes[:, halves[h]], y_scales[:, halves[h]], weights[:])

        def gather_values(t, bank):
            listed = held.tile([P, SLOTS], BF16, name="listed%d" % t, align_bytes=64)
            nc.vector.tensor_copy(out=listed[:], in_=value_pools[t][:].indirect(offsets[:]))
            words = listed[:].bitcast(F32)
            turned = banks.tile([P, 2, P], F32, name="turned", tag=bank)
            for u in range(2):
                nc.tensor.transpose(turned[:, u, :], words[:, u : 2 * P : 2], identity[:])
            return turned

        def regroup_values(t, turned):
            place = (2 * ROW, 2 * ROW + 1024, 3 * ROW, 4 * ROW + 1024)[t]
            grouped = shared.tile([P, P, PACK], BF16, name="v_bf%d" % t, offset=place, align_bytes=64)
            nc.scalar.copy(out=grouped[:].rearrange("p f t -> p (f t)").bitcast(F32).rearrange("p (f u) -> p f u", u=2),
                           in_=turned[:].rearrange("p u f -> p f u"))
            return grouped

        def quantise_values(t, grouped):
            quantise(value_codes[:, t, :], value_scales[:, t, :], grouped[:])

        def multiply(t, cols, result, bank):
            width = cols.stop - cols.start
            acc = banks.tile([P, width], F32, name="acc", tag=bank)
            nc.tensor.matmul_mx(out=acc[:], lhsT=value_codes[:, t, :].bitcast(FP8X4), lhsT_scale=value_scales[:, t, :],
                                rhs=y_codes[:, cols].bitcast(FP8X4), rhs_scale=y_scales[:, cols], start=True, stop=True)
            nc.vector.tensor_tensor(out=result[:, t, cols], in0=acc[:], in1=row_scale[:, cols], op=MULT)

        s0 = weigh(0)
        t0 = gather_values(0, "bank0")
        s1 = weigh(1)
        t1 = gather_values(1, "bank1")
        quantise_weights(0, sign_weights(0, s0))
        t2 = gather_values(2, "bank2")
        g0 = regroup_values(0, t0)
        g1 = regroup_values(1, t1)
        w1 = sign_weights(1, s1)
        quantise_values(0, g0)
        quantise_values(1, g1)
        quantise_weights(1, w1)
        t3 = gather_values(3, "bank3")
        g2 = regroup_values(2, t2)
        g3 = regroup_values(3, t3)
        quantise_values(2, g2)
        result = shared.tile([P, PACK, QUERIES], F32, name="result", offset=3 * ROW + 1024, align_bytes=64)
        every = slice(0, QUERIES)
        multiply(0, every, result, "bank4")
        multiply(1, every, result, "bank5")
        nc.sync.dma_start(out=out_rows[:, 0:2, :], in_=result[:, 0:2, :])
        quantise_values(3, g3)
        multiply(2, every, result, "bank6")
        nc.sync.dma_start(out=out_rows[:, 2, :], in_=result[:, 2, :])
        multiply(3, halves[0], result, "bank7")
        multiply(3, halves[1], result, "bank0")
        nc.sync.dma_start(out=out_rows[:, 3, :], in_=result[:, 3, :])

        out_codes = held.tile([P, QUERIES], I32, name="out_codes", align_bytes=64)
        out_scales = held.tile([P, QUERIES], U8, name="out_scales", align_bytes=64)
        rounded = held.tile([P, QUERIES, PACK], BF16, name="rounded", align_bytes=64)
        interleave(nc.scalar.copy, rounded[:, :SCALAR_SHARE, :], result[:, :, :SCALAR_SHARE])
        interleave(nc.vector.tensor_copy, rounded[:, SCALAR_SHARE:HALF, :], result[:, :, SCALAR_SHARE:HALF])
        interleave(nc.vector.tensor_copy, rounded[:, HALF:, :], result[:, :, HALF:])
        words_out = out_1[0].rearrange("p q t -> p (q t)").bitcast(I32)
        for cols in halves:
            quantise(out_codes[:, cols], out_scales[:, cols], rounded[:, cols, :])
            nc.sync.dma_start(out=words_out[:, cols], in_=out_codes[:, cols])
        for quad in range(4):
            engine = nc.scalar if quad % 2 == 0 else nc.sync
            engine.dma_start(out=out_2[0, 4 * quad : 4 * quad + 4, :].bitcast(I32),
                             in_=out_scales[32 * quad : 32 * quad + 4, :].bitcast(I32))
